import numpy as np
CORES = [5,6,7,13,14,15]
N = 6
H = 4
PERIODIC = True
def setup_inputs(rng):
    return {"x": rng.standard_normal((N, 128, 1024), dtype=np.float32)}
def reference(x):
    W = x.shape[2]
    y = np.zeros((N, 128, W + 2 * H), x.dtype)
    for r in range(N):
        y[r][:, H:H + W] = x[r]
        left, right = r - 1, r + 1
        if PERIODIC:
            left, right = left % N, right % N
        if 0 <= left < N:
            y[r][:, :H] = x[left][:, W - H:]
        if 0 <= right < N:
            y[r][:, W + H:] = x[right][:, :H]
    return {"y": y}

from concourse.bass import DstId, RemoteDMATransfer

H = 4

SCRATCH = {
    "edge": ("dram", [2, 128, H], "float32"),
    "halo": ("dram", [2, 128, H], "float32"),
    "hop": ("dram", [128, H], "float32"),
}
SEMAPHORES = ["packed", "sent", "left_in", "right_in", "hop_in", "stored"]

LOW, HIGH = 0x00FF, 0xFF00


def _via(src, topo):
    return topo.chip(src) * topo.CORES_PER_CHIP + 3


def _dst(core, topo):
    rid, pid, _ = topo.addr(core)
    return DstId(rid=rid, pnc=pid)


def rank_program(g, core, T, topo):
    cores = list(T.cores)
    n = len(cores)
    rank = T.rank_of(core)

    if rank is None:
        for r, src in enumerate(cores):
            left = cores[(r - 1) % n]
            if not topo.may_write(src, left) and _via(src, topo) == core:
                rid, pid, _ = topo.addr(left)
                g.wait_ge(T.sem.hop_in, 8)
                g.remote_dma(T.halo[1], T.hop[:], T.sem.right_in, T.sem.sent, pid, rid, LOW)
                g.wait_ge(T.sem.sent, 8)
        return

    W = T.x.shape[1]
    left, right = cores[(rank - 1) % n], cores[(rank + 1) % n]

    g.sync.dma_start(T.edge[0], T.x[:, 0:H]).then_inc(T.sem.packed, 16)
    g.scalar.dma_start(T.edge[1], T.x[:, W - H:W]).then_inc(T.sem.packed, 16)
    g.sync.dma_start(T.y[:, H:H + W], T.x[:]).then_inc(T.sem.stored, 16)

    if topo.may_write(core, left):
        to_left = (left, T.halo[1], T.sem.right_in)
    else:
        to_left = (_via(core, topo), T.hop[:], T.sem.hop_in)
    left_mask = HIGH if topo.chip(right) != topo.chip(core) else LOW
    g.wait_ge(T.sem.packed, 32)
    g.remote_dma_fused(
        [
            RemoteDMATransfer(dst_ids=[_dst(to_left[0], topo)], dma_engine_mask=left_mask, remote_sem=to_left[2],
                              src=T.edge[0], dst=to_left[1]),
            RemoteDMATransfer(dst_ids=[_dst(right, topo)], dma_engine_mask=LOW + HIGH - left_mask,
                              remote_sem=T.sem.left_in, src=T.edge[1], dst=T.halo[0]),
        ],
        local_sem=T.sem.sent,
    )

    g.sync.wait_ge(T.sem.left_in, 8)
    g.sync.dma_start(T.y[:, 0:H], T.halo[0]).then_inc(T.sem.stored, 16)
    g.scalar.wait_ge(T.sem.right_in, 8)
    g.scalar.dma_start(T.y[:, H + W:H + W + H], T.halo[1]).then_inc(T.sem.stored, 16)

    g.wait_ge(T.sem.sent, 16)
    g.wait_ge(T.sem.stored, 48)
